import numpy as np
import ml_dtypes


def mxq(x, axis, fmt="e4m3"):
    dtype, down = {"e4m3": (ml_dtypes.float8_e4m3fn, 7), "e5m2": (ml_dtypes.float8_e5m2, 14)}[fmt]
    v = np.moveaxis(np.asarray(x, np.float32).astype(ml_dtypes.bfloat16).astype(np.float64), axis, -1)
    blocks = v.reshape(v.shape[:-1] + (-1, 32))
    amax = np.abs(blocks).max(-1, keepdims=True)
    byte = np.maximum(np.where(amax > 0, np.frexp(amax)[1] - 1 + 127, 0) - down, 1)
    scale = np.exp2(byte - 127.0)
    codes = (blocks / scale).astype(np.float32).astype(dtype).astype(np.float64)
    return np.moveaxis((codes * scale).reshape(v.shape), -1, axis)


WIDE = False


def mx_kscale(k):
    if not WIDE:
        return np.ones(k)
    levels = np.array([10, -10, 5, -5, 0])
    if k % 512:
        return np.exp2(np.random.permutation(np.resize(levels, k // 32))).repeat(32)
    a = np.empty((k // 512, 16))
    for p in range(k // 512):
        a[p, :8] = np.random.permutation(np.resize(levels, 8))
        for g in range(8):
            far = levels[np.abs(levels - a[p, g]) >= 10]
            a[p, g + 8] = far[np.random.randint(len(far))]
    return np.exp2(a.ravel()).repeat(32)


def f64(x):
    return np.asarray(x).astype(np.float64)


def striped(idx):
    return np.tile(idx.reshape(-1, 16).T, (8, 1)).astype(np.uint16)


def unstriped(offs):
    return offs[:16].T.reshape(-1).astype(np.int64)


E2M1 = np.array([0.0, 0.5, 1.0, 1.5, 2.0, 3.0, 4.0, 6.0, -0.0, -0.5, -1.0, -1.5, -2.0, -3.0, -4.0, -6.0])


def pack_fp4(w):
    k, n = w.shape
    w = f64(np.asarray(w, np.float32).astype(ml_dtypes.bfloat16)).reshape(k // 32, 32, n)
    amax = np.abs(w).max(1)
    mant, ex = np.frexp(amax / 6.0)
    byte = np.clip(np.where(amax > 0, np.where(mant > 0.5, ex, ex - 1) + 127, 1), 1, 254)
    scaled = (w * np.exp2(127.0 - byte)[:, None, :]).reshape(k, n).astype(np.float32)
    c = np.ascontiguousarray(scaled.reshape(k // 512, 128, 4, n).transpose(0, 1, 3, 2)).astype(ml_dtypes.float4_e2m1fn).view(np.uint8) & 0xF
    words = (c[..., 0::2] | (c[..., 1::2] << 4)).reshape(k // 512, 128, 2 * n)
    return np.ascontiguousarray(words), np.ascontiguousarray(byte.astype(np.uint8).reshape(k // 512, 16, n))


def unpack_fp4(words, scales):
    g, _, n = scales.shape
    words = np.ascontiguousarray(words).reshape(g, 128, n, 2)
    nib = np.empty((g, 128, n, 4), np.uint8)
    nib[..., 0::2] = words & 0xF
    nib[..., 1::2] = words >> 4
    vals = E2M1[nib] * np.repeat(np.exp2(scales.astype(np.float64) - 127.0), 8, axis=1)[..., None]
    return vals.transpose(0, 1, 3, 2).reshape(g * 512, n)


def relu(v):
    return np.maximum(v, 0.0)


K, T, D, N = 1024, 512, 4, 128
P = 2 ** 7


def setup_inputs():
    n = np.random.standard_normal
    s = mx_kscale(K)[:, None]
    packed_xT = pack_fp4(n((K, T)) * s)
    return {
        "x_words": packed_xT[0],
        "x_scales": packed_xT[1],
        "w1": (n((K, N)) / np.sqrt(K) / s).astype(np.float32),
        "gate": (np.tile(np.random.uniform(0.2, 1.0, (D, 1, T)) / np.sqrt(D), (1, P, 1))).astype(np.float32),
        "pos1": striped(np.random.permutation(T)),
        "pos2": striped(np.random.permutation(T)),
        "pos3": striped(np.random.permutation(T)),
        "pos4": striped(np.random.permutation(T)),
    }


def reference(x_words, x_scales, w1, gate, pos1, pos2, pos3, pos4):
    xq = unpack_fp4(x_words, x_scales)
    y = relu(mxq(f64(w1), 0, "e4m3").T @ xq)
    return y + (y[:, unstriped(pos1)] - y) * f64(gate)[0, :1] + (y[:, unstriped(pos2)] - y) * f64(gate)[1, :1] + (y[:, unstriped(pos3)] - y) * f64(gate)[2, :1] + (y[:, unstriped(pos4)] - y) * f64(gate)[3, :1]

@@ -1,0 +1,161 @@
+from contextlib import ExitStack
+
+import concourse.mybir as mybir
+from concourse.masks import make_identity
+
+K, T, D, N = 1024, 512, 4, 128
+FLOPS = 2 * K * T * N
+
+F32 = mybir.dt.float32
+BF16 = mybir.dt.bfloat16
+I32 = mybir.dt.int32
+U32 = mybir.dt.uint32
+U16 = mybir.dt.uint16
+U8 = mybir.dt.uint8
+FP8X4 = mybir.dt.float8_e4m3fn_x4
+FP4X4 = mybir.dt.float4_e2m1fn_x4
+ALU = mybir.AluOpType
+ACT = mybir.ActivationFunctionType
+AXIS = mybir.AxisListType
+
+P = 128
+PACK = 4
+PASSES = K // (P * PACK)
+BLOCKS = T // P
+HALF = T // 2
+
+
+def tile_picked_wgrand_relu_l_kernel(
+    tc, x_words, x_scales, w1, gate, pos1, pos2, pos3, pos4, out
+):
+    nc = tc.nc
+    with ExitStack() as ctx:
+        keep = ctx.enter_context(tc.tile_pool(name="keep", bufs=1))
+        psum = ctx.enter_context(tc.psum_pool(name="psum", bufs=1))
+
+        grow = keep.tile([P, P], F32, name="grow")
+        nc.gpsimd.memset(grow[:], 0.0)
+        nc.scalar.dma_start(
+            out=grow[0 : D * BLOCKS, :],
+            in_=gate[:, 0, :].rearrange("d (b p) -> d b p", p=P),
+        )
+        xs = keep.tile([P, PASSES, T], U8, align_bytes=64, name="xs")
+        nc.gpsimd.memset(xs[:].rearrange("p z c -> p (z c)").bitcast(I32), 0)
+        warm = keep.tile([P, 2], F32, name="warm")
+        nc.gpsimd.memset(warm[:, 0:1], 0.0)
+        nc.scalar.activation(warm[:, 1:2], warm[:, 0:1], ACT.Relu)
+        ident = keep.tile([P, P], F32, name="ident")
+        make_identity(nc, ident[:])
+
+        raw = [keep.tile([P, PACK, N], F32, name=f"raw{z}") for z in range(PASSES)]
+        for z in range(PASSES):
+            rows = w1[z * P * PACK : (z + 1) * P * PACK, :]
+            nc.sync.dma_start(out=raw[z][:], in_=rows.rearrange("(p j) n -> p j n", j=PACK))
+        xw = keep.tile([P, PASSES, 2 * T], U8, align_bytes=64, name="xw")
+        nc.sync.dma_start(out=xw[:].bitcast(I32), in_=x_words.bitcast(I32).rearrange("z p c -> p z c"))
+        for q in range(4):
+            nc.sync.dma_start(
+                out=xs[32 * q : 32 * q + 4, :, :].bitcast(I32),
+                in_=x_scales.bitcast(I32)[:, 4 * q : 4 * q + 4, :].rearrange("z r c -> r z c"),
+            )
+        lists = []
+        for d, pos in enumerate((pos1, pos2, pos3, pos4)):
+            offsets = keep.tile([P, T // 16], U16, name=f"list{d}")
+            nc.sync.dma_start(offsets[:], pos)
+            lists.append(offsets)
+        wide = {}
+        for d in (2, 3):
+            wide[d] = keep.tile([P, T], F32, name=f"wide{d}")
+            nc.sync.dma_start(out=wide[d][:], in_=gate[d])
+
+        acc = [psum.tile([P, P], F32, name=f"acc{b}") for b in range(BLOCKS)]
+        turn = [psum.tile([P, 3, P], F32, name=f"turn{b}") for b in range(BLOCKS)]
+
+        grouped = [keep.tile([P, N, PACK], BF16, align_bytes=64, name=f"grouped{z}") for z in range(PASSES)]
+        codes = [keep.tile([P, N], U32, align_bytes=64, name=f"codes{z}") for z in range(PASSES)]
+        ws = [keep.tile([P, N], U8, align_bytes=64, name=f"ws{z}") for z in range(PASSES)]
+        for z in range(PASSES):
+            src = raw[z][:].rearrange("p j (c i) -> p c j i", i=4)
+            dst = grouped[z][:].rearrange("p (c i) j -> p c j i", i=4)
+            if z == 0:
+                nc.vector.tensor_copy(out=dst, in_=src)
+            else:
+                nc.scalar.copy(out=dst, in_=src)
+            nc.vector.quantize_mx(
+                out=codes[z][:].bitcast(FP8X4),
+                scales=ws[z][:],
+                in_=grouped[z][:].rearrange("p n j -> p (n j)"),
+            )
+
+        nc.tensor.transpose(acc[3][:], grow[:], ident[:])
+        gcol = keep.tile([P, D, BLOCKS], F32, name="gcol")
+        nc.vector.tensor_copy(out=gcol[:].rearrange("p d b -> p (d b)"), in_=acc[3][:, 0 : D * BLOCKS])
+        gsum = keep.tile([P, BLOCKS], F32, name="gsum")
+        nc.vector.tensor_reduce(out=gsum[:], in_=gcol[:].rearrange("p d b -> p b d"), axis=AXIS.X, op=ALU.add)
+        stay = keep.tile([P, BLOCKS], F32, name="stay")
+        nc.vector.tensor_scalar(stay[:], gsum[:], -1.0, 1.0, ALU.mult, ALU.add)
+
+        for z in range(PASSES):
+            for b in range(BLOCKS):
+                nc.tensor.matmul_mx(
+                    out=acc[b][:],
+                    lhsT=codes[z][:].bitcast(FP8X4),
+                    lhsT_scale=ws[z][:],
+                    rhs=xw[:, z, 2 * P * b : 2 * P * (b + 1)].bitcast(FP4X4),
+                    rhs_scale=xs[:, z, P * b : P * (b + 1)],
+                    start=(z == 0),
+                    stop=(z == PASSES - 1),
+                )
+        y = keep.tile([P, T], F32, name="y")
+        for b in range(BLOCKS):
+            cols = slice(P * b, P * (b + 1))
+            if b % 2 == 0:
+                nc.vector.tensor_scalar_max(y[:, cols], acc[b][:], 0.0)
+            else:
+                nc.scalar.activation(y[:, cols], acc[b][:], ACT.Relu)
+
+        scaled = keep.tile([P, 3, BLOCKS, P], F32, name="scaled")
+
+        def through_tensor(term, src, factor, blocks):
+            for b in blocks:
+                nc.tensor.transpose(turn[b][:, term, :], src[:, P * b : P * (b + 1)], ident[:])
+                nc.scalar.activation(scaled[:, term, b, :], turn[b][:, term, :], ACT.Copy, scale=factor[:, b : b + 1])
+            for b in blocks:
+                nc.tensor.matmul(
+                    acc[b][:], scaled[:, term, b, :], ident[:],
+                    start=(term == 0), stop=(term == 2), is_transpose=True,
+                )
+
+        through_tensor(0, y, stay, range(BLOCKS))
+        got = [keep.tile([P, T], F32, name=f"got{d}") for d in range(D)]
+        for d in (0, 1):
+            for h in range(2):
+                cols = slice(HALF * h, HALF * (h + 1))
+                offs = lists[d][:, HALF * h // 16 : HALF * (h + 1) // 16]
+                nc.vector.tensor_copy(got[d][:, cols], y[:].indirect(offs))
+                through_tensor(1 + d, got[d], gcol[:, d, :], (2 * h, 2 * h + 1))
+
+        def product(d, lo, hi):
+            offs = lists[d][:, lo // 16 : hi // 16]
+            nc.vector.tensor_tensor(got[d][:, lo:hi], y[:].indirect(offs), wide[d][:, lo:hi], ALU.mult)
+
+        part = keep.tile([P, T], F32, name="part")
+        res = keep.tile([P, T], F32, name="res")
+        product(2, 0, HALF)
+        product(3, 0, HALF)
+        product(2, HALF, T)
+        nc.vector.tensor_tensor(part[:, 0:HALF], got[2][:, 0:HALF], got[3][:, 0:HALF], ALU.add)
+        for b in (0, 1):
+            cols = slice(P * b, P * (b + 1))
+            nc.vector.tensor_tensor(res[:, cols], acc[b][:], part[:, cols], ALU.add)
+        nc.sync.dma_start(out=out[:, 0:HALF], in_=res[:, 0:HALF])
+        for b in (2, 3):
+            cols = slice(P * b, P * (b + 1))
+            nc.vector.tensor_tensor(part[:, cols], acc[b][:], got[2][:, cols], ALU.add)
+        for b in (2, 3):
+            product(3, P * b, P * (b + 1))
+        for b in (2, 3):
+            cols = slice(P * b, P * (b + 1))
+            nc.vector.tensor_tensor(res[:, cols], part[:, cols], got[3][:, cols], ALU.add)
+            queue = nc.scalar if b == 2 else nc.sync
+            queue.dma_start(out=out[:, cols], in_=res[:, cols])

@@ -23,6 +23,7 @@ PACK = 4
 PASSES = K // (P * PACK)
 BLOCKS = T // P
 HALF = T // 2
+SPLIT = 20
 
 
 def tile_picked_wgrand_relu_l_kernel(
@@ -33,14 +34,14 @@ def tile_picked_wgrand_relu_l_kernel(
         keep = ctx.enter_context(tc.tile_pool(name="keep", bufs=1))
         psum = ctx.enter_context(tc.psum_pool(name="psum", bufs=1))
 
-        grow = keep.tile([P, P], F32, name="grow")
+        grow = keep.tile([P, P], F32, align_bytes=64, name="grow", tag="codes0")
         nc.gpsimd.memset(grow[:], 0.0)
+        xs = keep.tile([P, PASSES, T], U8, align_bytes=64, name="xs")
+        nc.vector.memset(xs[:].rearrange("p z c -> p (z c)").bitcast(I32), 0)
         nc.scalar.dma_start(
             out=grow[0 : D * BLOCKS, :],
             in_=gate[:, 0, :].rearrange("d (b p) -> d b p", p=P),
         )
-        xs = keep.tile([P, PASSES, T], U8, align_bytes=64, name="xs")
-        nc.gpsimd.memset(xs[:].rearrange("p z c -> p (z c)").bitcast(I32), 0)
         warm = keep.tile([P, 2], F32, name="warm")
         nc.gpsimd.memset(warm[:, 0:1], 0.0)
         nc.scalar.activation(warm[:, 1:2], warm[:, 0:1], ACT.Relu)
@@ -51,13 +52,13 @@ def tile_picked_wgrand_relu_l_kernel(
         for z in range(PASSES):
             rows = w1[z * P * PACK : (z + 1) * P * PACK, :]
             nc.sync.dma_start(out=raw[z][:], in_=rows.rearrange("(p j) n -> p j n", j=PACK))
-        xw = keep.tile([P, PASSES, 2 * T], U8, align_bytes=64, name="xw")
-        nc.sync.dma_start(out=xw[:].bitcast(I32), in_=x_words.bitcast(I32).rearrange("z p c -> p z c"))
         for q in range(4):
             nc.sync.dma_start(
                 out=xs[32 * q : 32 * q + 4, :, :].bitcast(I32),
                 in_=x_scales.bitcast(I32)[:, 4 * q : 4 * q + 4, :].rearrange("z r c -> r z c"),
             )
+        xw = keep.tile([P, PASSES, 2 * T], U8, align_bytes=64, name="xw")
+        nc.sync.dma_start(out=xw[:].bitcast(I32), in_=x_words.bitcast(I32).rearrange("z p c -> p z c"))
         lists = []
         for d, pos in enumerate((pos1, pos2, pos3, pos4)):
             offsets = keep.tile([P, T // 16], U16, name=f"list{d}")
@@ -71,25 +72,23 @@ def tile_picked_wgrand_relu_l_kernel(
         acc = [psum.tile([P, P], F32, name=f"acc{b}") for b in range(BLOCKS)]
         turn = [psum.tile([P, 3, P], F32, name=f"turn{b}") for b in range(BLOCKS)]
 
+        nc.tensor.transpose(turn[3][:, 2, :], grow[:], ident[:])
         grouped = [keep.tile([P, N, PACK], BF16, align_bytes=64, name=f"grouped{z}") for z in range(PASSES)]
         codes = [keep.tile([P, N], U32, align_bytes=64, name=f"codes{z}") for z in range(PASSES)]
         ws = [keep.tile([P, N], U8, align_bytes=64, name=f"ws{z}") for z in range(PASSES)]
         for z in range(PASSES):
             src = raw[z][:].rearrange("p j (c i) -> p c j i", i=4)
             dst = grouped[z][:].rearrange("p (c i) j -> p c j i", i=4)
-            if z == 0:
-                nc.vector.tensor_copy(out=dst, in_=src)
-            else:
-                nc.scalar.copy(out=dst, in_=src)
+            nc.vector.tensor_copy(out=dst[:, :SPLIT], in_=src[:, :SPLIT])
+            nc.scalar.copy(out=dst[:, SPLIT:], in_=src[:, SPLIT:])
             nc.vector.quantize_mx(
                 out=codes[z][:].bitcast(FP8X4),
                 scales=ws[z][:],
                 in_=grouped[z][:].rearrange("p n j -> p (n j)"),
             )
 
-        nc.tensor.transpose(acc[3][:], grow[:], ident[:])
         gcol = keep.tile([P, D, BLOCKS], F32, name="gcol")
-        nc.vector.tensor_copy(out=gcol[:].rearrange("p d b -> p (d b)"), in_=acc[3][:, 0 : D * BLOCKS])
+        nc.scalar.copy(out=gcol[:].rearrange("p d b -> p (d b)"), in_=turn[3][:, 2, 0 : D * BLOCKS])
         gsum = keep.tile([P, BLOCKS], F32, name="gsum")
         nc.vector.tensor_reduce(out=gsum[:], in_=gcol[:].rearrange("p d b -> p b d"), axis=AXIS.X, op=ALU.add)
         stay = keep.tile([P, BLOCKS], F32, name="stay")

@@ -16,145 +16,148 @@ FP8X4 = mybir.dt.float8_e4m3fn_x4
 FP4X4 = mybir.dt.float4_e2m1fn_x4
 ALU = mybir.AluOpType
 ACT = mybir.ActivationFunctionType
-AXIS = mybir.AxisListType
 
 P = 128
 PACK = 4
 PASSES = K // (P * PACK)
+QUADRANTS = 4
 BLOCKS = T // P
-HALF = T // 2
-SPLIT = 20
+PER_COLUMN = 16
+RUN = 4
+VECTOR_RUNS = 20
 
 
 def tile_picked_wgrand_relu_l_kernel(
     tc, x_words, x_scales, w1, gate, pos1, pos2, pos3, pos4, out
 ):
     nc = tc.nc
+
+    def block(b):
+        return slice(P * b, P * (b + 1))
+
     with ExitStack() as ctx:
         keep = ctx.enter_context(tc.tile_pool(name="keep", bufs=1))
         psum = ctx.enter_context(tc.psum_pool(name="psum", bufs=1))
 
-        grow = keep.tile([P, P], F32, align_bytes=64, name="grow", tag="codes0")
-        nc.gpsimd.memset(grow[:], 0.0)
-        xs = keep.tile([P, PASSES, T], U8, align_bytes=64, name="xs")
-        nc.vector.memset(xs[:].rearrange("p z c -> p (z c)").bitcast(I32), 0)
-        nc.scalar.dma_start(
-            out=grow[0 : D * BLOCKS, :],
-            in_=gate[:, 0, :].rearrange("d (b p) -> d b p", p=P),
-        )
-        warm = keep.tile([P, 2], F32, name="warm")
-        nc.gpsimd.memset(warm[:, 0:1], 0.0)
-        nc.scalar.activation(warm[:, 1:2], warm[:, 0:1], ACT.Relu)
+        x_scale = keep.tile([P, PASSES, T], U8, align_bytes=64, name="x_scale")
+        nc.vector.memset(x_scale[:].rearrange("p z c -> p (z c)").bitcast(I32), 0)
+        zero = keep.tile([P, 1], F32, name="zero")
+        nc.gpsimd.memset(zero[:], 0.0)
+        gate_rows = keep.tile([P, P], F32, name="gate_rows")
+        nc.scalar.activation(gate_rows[:], zero[:].to_broadcast([P, P]), ACT.Relu)
         ident = keep.tile([P, P], F32, name="ident")
         make_identity(nc, ident[:])
 
-        raw = [keep.tile([P, PACK, N], F32, name=f"raw{z}") for z in range(PASSES)]
+        w_raw = [keep.tile([P, PACK, N], F32, name=f"w_raw{z}") for z in range(PASSES)]
         for z in range(PASSES):
             rows = w1[z * P * PACK : (z + 1) * P * PACK, :]
-            nc.sync.dma_start(out=raw[z][:], in_=rows.rearrange("(p j) n -> p j n", j=PACK))
-        for q in range(4):
+            nc.sync.dma_start(out=w_raw[z][:], in_=rows.rearrange("(p t) n -> p t n", t=PACK))
+        for q in range(QUADRANTS):
             nc.sync.dma_start(
-                out=xs[32 * q : 32 * q + 4, :, :].bitcast(I32),
+                out=x_scale[32 * q : 32 * q + 4, :, :].bitcast(I32),
                 in_=x_scales.bitcast(I32)[:, 4 * q : 4 * q + 4, :].rearrange("z r c -> r z c"),
             )
-        xw = keep.tile([P, PASSES, 2 * T], U8, align_bytes=64, name="xw")
-        nc.sync.dma_start(out=xw[:].bitcast(I32), in_=x_words.bitcast(I32).rearrange("z p c -> p z c"))
-        lists = []
+        x_codes = [keep.tile([P, 2 * T], U8, align_bytes=64, name=f"x_codes{z}") for z in range(PASSES)]
+        for z in range(PASSES):
+            nc.sync.dma_start(out=x_codes[z][:].bitcast(I32), in_=x_words.bitcast(I32)[z])
+        gates, lists = [], []
         for d, pos in enumerate((pos1, pos2, pos3, pos4)):
-            offsets = keep.tile([P, T // 16], U16, name=f"list{d}")
+            gate_tile = keep.tile([P, T], F32, name=f"gate{d}")
+            nc.sync.dma_start(out=gate_tile[:], in_=gate[d])
+            gates.append(gate_tile)
+            offsets = keep.tile([P, T // PER_COLUMN], U16, name=f"list{d}")
             nc.sync.dma_start(offsets[:], pos)
             lists.append(offsets)
-        wide = {}
-        for d in (2, 3):
-            wide[d] = keep.tile([P, T], F32, name=f"wide{d}")
-            nc.sync.dma_start(out=wide[d][:], in_=gate[d])
+            if d == 0:
+                nc.sync.dma_start(
+                    out=gate_rows[0 : D * BLOCKS, :],
+                    in_=gate[:, 0, :].rearrange("e (b p) -> e b p", p=P),
+                )
 
-        acc = [psum.tile([P, P], F32, name=f"acc{b}") for b in range(BLOCKS)]
-        turn = [psum.tile([P, 3, P], F32, name=f"turn{b}") for b in range(BLOCKS)]
+        acc = [psum.tile([P, 3, P], F32, name=f"acc{b}") for b in range(BLOCKS)]
+        turn = [psum.tile([P, P], F32, name=f"turn{b}") for b in range(BLOCKS)]
 
-        nc.tensor.transpose(turn[3][:, 2, :], grow[:], ident[:])
-        grouped = [keep.tile([P, N, PACK], BF16, align_bytes=64, name=f"grouped{z}") for z in range(PASSES)]
-        codes = [keep.tile([P, N], U32, align_bytes=64, name=f"codes{z}") for z in range(PASSES)]
-        ws = [keep.tile([P, N], U8, align_bytes=64, name=f"ws{z}") for z in range(PASSES)]
+        w_bf16 = [keep.tile([P, N, PACK], BF16, align_bytes=64, name=f"w_bf16{z}") for z in range(PASSES)]
+        w_codes = [keep.tile([P, N], U32, align_bytes=64, name=f"w_codes{z}") for z in range(PASSES)]
+        w_scale = [keep.tile([P, N], U8, align_bytes=64, name=f"w_scale{z}") for z in range(PASSES)]
         for z in range(PASSES):
-            src = raw[z][:].rearrange("p j (c i) -> p c j i", i=4)
-            dst = grouped[z][:].rearrange("p (c i) j -> p c j i", i=4)
-            nc.vector.tensor_copy(out=dst[:, :SPLIT], in_=src[:, :SPLIT])
-            nc.scalar.copy(out=dst[:, SPLIT:], in_=src[:, SPLIT:])
+            src = w_raw[z][:].rearrange("p t (c i) -> p c t i", i=RUN)
+            dst = w_bf16[z][:].rearrange("p (c i) t -> p c t i", i=RUN)
+            nc.vector.tensor_copy(out=dst[:, :VECTOR_RUNS], in_=src[:, :VECTOR_RUNS])
+            nc.scalar.copy(out=dst[:, VECTOR_RUNS:], in_=src[:, VECTOR_RUNS:])
             nc.vector.quantize_mx(
-                out=codes[z][:].bitcast(FP8X4),
-                scales=ws[z][:],
-                in_=grouped[z][:].rearrange("p n j -> p (n j)"),
+                out=w_codes[z][:].bitcast(FP8X4),
+                scales=w_scale[z][:],
+                in_=w_bf16[z][:].rearrange("p n t -> p (n t)"),
             )
-
-        gcol = keep.tile([P, D, BLOCKS], F32, name="gcol")
-        nc.scalar.copy(out=gcol[:].rearrange("p d b -> p (d b)"), in_=turn[3][:, 2, 0 : D * BLOCKS])
-        gsum = keep.tile([P, BLOCKS], F32, name="gsum")
-        nc.vector.tensor_reduce(out=gsum[:], in_=gcol[:].rearrange("p d b -> p b d"), axis=AXIS.X, op=ALU.add)
-        stay = keep.tile([P, BLOCKS], F32, name="stay")
-        nc.vector.tensor_scalar(stay[:], gsum[:], -1.0, 1.0, ALU.mult, ALU.add)
 
         for z in range(PASSES):
             for b in range(BLOCKS):
                 nc.tensor.matmul_mx(
-                    out=acc[b][:],
-                    lhsT=codes[z][:].bitcast(FP8X4),
-                    lhsT_scale=ws[z][:],
-                    rhs=xw[:, z, 2 * P * b : 2 * P * (b + 1)].bitcast(FP4X4),
-                    rhs_scale=xs[:, z, P * b : P * (b + 1)],
+                    out=acc[b][:, 0, :],
+                    lhsT=w_codes[z][:].bitcast(FP8X4),
+                    lhsT_scale=w_scale[z][:],
+                    rhs=x_codes[z][:, 2 * P * b : 2 * P * (b + 1)].bitcast(FP4X4),
+                    rhs_scale=x_scale[:, z, block(b)],
                     start=(z == 0),
                     stop=(z == PASSES - 1),
                 )
         y = keep.tile([P, T], F32, name="y")
         for b in range(BLOCKS):
-            cols = slice(P * b, P * (b + 1))
             if b % 2 == 0:
-                nc.vector.tensor_scalar_max(y[:, cols], acc[b][:], 0.0)
+                nc.vector.tensor_scalar_max(y[:, block(b)], acc[b][:, 0, :], 0.0)
             else:
-                nc.scalar.activation(y[:, cols], acc[b][:], ACT.Relu)
+                nc.scalar.activation(y[:, block(b)], acc[b][:, 0, :], ACT.Relu)
 
-        scaled = keep.tile([P, 3, BLOCKS, P], F32, name="scaled")
+        last = BLOCKS - 1
+        nc.tensor.transpose(acc[last][:, 2, :], gate_rows[:], ident[:])
+        gate_cols = acc[last][:, 2, 0 : D * BLOCKS].rearrange("p (e b) -> p b e", e=D)
+        summands = keep.tile([P, BLOCKS, D], F32, name="summands")
+        stay = keep.tile([P, BLOCKS], F32, name="stay")
+        for b in range(BLOCKS):
+            nc.scalar.activation(
+                summands[:, b, :], gate_cols[:, b, :], ACT.Copy,
+                bias=1.0 / D, scale=-1.0, accum_out=stay[:, b : b + 1],
+            )
 
-        def through_tensor(term, src, factor, blocks):
+        own = keep.tile([P, BLOCKS, P], F32, name="own")
+        for b in range(BLOCKS):
+            nc.tensor.transpose(acc[b][:, 1, :], y[:, block(b)], ident[:])
+            nc.scalar.activation(own[:, b, :], acc[b][:, 1, :], ACT.Copy, scale=stay[:, b : b + 1])
+        for b in range(BLOCKS):
+            nc.tensor.matmul(acc[b][:, 0, :], own[:, b, :], ident[:], start=True, stop=False, is_transpose=True)
+
+        pulled = [keep.tile([P, T], F32, name=f"pulled{d}") for d in range(D)]
+
+        def pull(d, blocks):
+            lo, hi = P * blocks[0], P * (blocks[-1] + 1)
+            offsets = lists[d][:, lo // PER_COLUMN : hi // PER_COLUMN]
+            nc.vector.tensor_tensor(pulled[d][:, lo:hi], y[:].indirect(offsets), gates[d][:, lo:hi], ALU.mult)
+
+        halves = [(0, 1), (2, 3)]
+        for d in range(D - 1):
+            for blocks in halves if d < D - 2 else [(0, 1), (2,), (3,)]:
+                pull(d, blocks)
+                for b in blocks:
+                    nc.tensor.matmul(
+                        turn[b][:], pulled[d][:, block(b)], ident[:],
+                        start=(d == 0), stop=(d == D - 2), is_transpose=True,
+                    )
+        three = keep.tile([P, BLOCKS, P], F32, name="three")
+        for b in range(BLOCKS):
+            nc.scalar.copy(three[:, b, :], turn[b][:])
+            nc.tensor.matmul(acc[b][:, 0, :], three[:, b, :], ident[:], start=False, stop=True, is_transpose=True)
+
+        for blocks in halves:
+            pull(D - 1, blocks)
+        result = keep.tile([P, T], F32, name="result")
+
+        def finish(blocks, queue):
             for b in blocks:
-                nc.tensor.transpose(turn[b][:, term, :], src[:, P * b : P * (b + 1)], ident[:])
-                nc.scalar.activation(scaled[:, term, b, :], turn[b][:, term, :], ACT.Copy, scale=factor[:, b : b + 1])
-            for b in blocks:
-                nc.tensor.matmul(
-                    acc[b][:], scaled[:, term, b, :], ident[:],
-                    start=(term == 0), stop=(term == 2), is_transpose=True,
-                )
+                nc.vector.tensor_tensor(result[:, block(b)], acc[b][:, 0, :], pulled[D - 1][:, block(b)], ALU.add)
+            cols = slice(P * blocks[0], P * (blocks[-1] + 1))
+            queue.dma_start(out=out[:, cols], in_=result[:, cols])
 
-        through_tensor(0, y, stay, range(BLOCKS))
-        got = [keep.tile([P, T], F32, name=f"got{d}") for d in range(D)]
-        for d in (0, 1):
-            for h in range(2):
-                cols = slice(HALF * h, HALF * (h + 1))
-                offs = lists[d][:, HALF * h // 16 : HALF * (h + 1) // 16]
-                nc.vector.tensor_copy(got[d][:, cols], y[:].indirect(offs))
-                through_tensor(1 + d, got[d], gcol[:, d, :], (2 * h, 2 * h + 1))
-
-        def product(d, lo, hi):
-            offs = lists[d][:, lo // 16 : hi // 16]
-            nc.vector.tensor_tensor(got[d][:, lo:hi], y[:].indirect(offs), wide[d][:, lo:hi], ALU.mult)
-
-        part = keep.tile([P, T], F32, name="part")
-        res = keep.tile([P, T], F32, name="res")
-        product(2, 0, HALF)
-        product(3, 0, HALF)
-        product(2, HALF, T)
-        nc.vector.tensor_tensor(part[:, 0:HALF], got[2][:, 0:HALF], got[3][:, 0:HALF], ALU.add)
-        for b in (0, 1):
-            cols = slice(P * b, P * (b + 1))
-            nc.vector.tensor_tensor(res[:, cols], acc[b][:], part[:, cols], ALU.add)
-        nc.sync.dma_start(out=out[:, 0:HALF], in_=res[:, 0:HALF])
-        for b in (2, 3):
-            cols = slice(P * b, P * (b + 1))
-            nc.vector.tensor_tensor(part[:, cols], acc[b][:], got[2][:, cols], ALU.add)
-        for b in (2, 3):
-            product(3, P * b, P * (b + 1))
-        for b in (2, 3):
-            cols = slice(P * b, P * (b + 1))
-            nc.vector.tensor_tensor(res[:, cols], part[:, cols], got[3][:, cols], ALU.add)
-            queue = nc.scalar if b == 2 else nc.sync
-            queue.dma_start(out=out[:, cols], in_=res[:, cols])
+        finish((0, 1), nc.sync)
+        finish((2,), nc.scalar)
+        finish((3,), nc.sync)

from contextlib import ExitStack

import concourse.mybir as mybir
from concourse.masks import make_identity

K, T, D, N = 1024, 512, 4, 128
FLOPS = 2 * K * T * N

F32 = mybir.dt.float32
BF16 = mybir.dt.bfloat16
I32 = mybir.dt.int32
U32 = mybir.dt.uint32
U16 = mybir.dt.uint16
U8 = mybir.dt.uint8
FP8X4 = mybir.dt.float8_e4m3fn_x4
FP4X4 = mybir.dt.float4_e2m1fn_x4
ALU = mybir.AluOpType
ACT = mybir.ActivationFunctionType

P = 128
PACK = 4
PASSES = K // (P * PACK)
QUADRANTS = 4
BLOCKS = T // P
PER_COLUMN = 16
RUN = 4
VECTOR_RUNS = 20


def tile_picked_wgrand_relu_l_kernel(
    tc, x_words, x_scales, w1, gate, pos1, pos2, pos3, pos4, out
):
    nc = tc.nc

    def block(b):
        return slice(P * b, P * (b + 1))

    with ExitStack() as ctx:
        keep = ctx.enter_context(tc.tile_pool(name="keep", bufs=1))
        psum = ctx.enter_context(tc.psum_pool(name="psum", bufs=1))

        x_scale = keep.tile([P, PASSES, T], U8, align_bytes=64, name="x_scale")
        nc.vector.memset(x_scale[:].rearrange("p z c -> p (z c)").bitcast(I32), 0)
        zero = keep.tile([P, 1], F32, name="zero")
        nc.gpsimd.memset(zero[:], 0.0)
        gate_rows = keep.tile([P, P], F32, name="gate_rows")
        nc.scalar.activation(gate_rows[:], zero[:].to_broadcast([P, P]), ACT.Relu)
        ident = keep.tile([P, P], F32, name="ident")
        make_identity(nc, ident[:])

        w_raw = [keep.tile([P, PACK, N], F32, name=f"w_raw{z}") for z in range(PASSES)]
        for z in range(PASSES):
            rows = w1[z * P * PACK : (z + 1) * P * PACK, :]
            nc.sync.dma_start(out=w_raw[z][:], in_=rows.rearrange("(p t) n -> p t n", t=PACK))
        for q in range(QUADRANTS):
            nc.sync.dma_start(
                out=x_scale[32 * q : 32 * q + 4, :, :].bitcast(I32),
                in_=x_scales.bitcast(I32)[:, 4 * q : 4 * q + 4, :].rearrange("z r c -> r z c"),
            )
        x_codes = [keep.tile([P, 2 * T], U8, align_bytes=64, name=f"x_codes{z}") for z in range(PASSES)]
        for z in range(PASSES):
            nc.sync.dma_start(out=x_codes[z][:].bitcast(I32), in_=x_words.bitcast(I32)[z])
        gates, lists = [], []
        for d, pos in enumerate((pos1, pos2, pos3, pos4)):
            gate_tile = keep.tile([P, T], F32, name=f"gate{d}")
            nc.sync.dma_start(out=gate_tile[:], in_=gate[d])
            gates.append(gate_tile)
            offsets = keep.tile([P, T // PER_COLUMN], U16, name=f"list{d}")
            nc.sync.dma_start(offsets[:], pos)
            lists.append(offsets)
            if d == 0:
                nc.sync.dma_start(
                    out=gate_rows[0 : D * BLOCKS, :],
                    in_=gate[:, 0, :].rearrange("e (b p) -> e b p", p=P),
                )

        acc = [psum.tile([P, 3, P], F32, name=f"acc{b}") for b in range(BLOCKS)]
        turn = [psum.tile([P, P], F32, name=f"turn{b}") for b in range(BLOCKS)]

        w_bf16 = [keep.tile([P, N, PACK], BF16, align_bytes=64, name=f"w_bf16{z}") for z in range(PASSES)]
        w_codes = [keep.tile([P, N], U32, align_bytes=64, name=f"w_codes{z}") for z in range(PASSES)]
        w_scale = [keep.tile([P, N], U8, align_bytes=64, name=f"w_scale{z}") for z in range(PASSES)]
        for z in range(PASSES):
            src = w_raw[z][:].rearrange("p t (c i) -> p c t i", i=RUN)
            dst = w_bf16[z][:].rearrange("p (c i) t -> p c t i", i=RUN)
            nc.vector.tensor_copy(out=dst[:, :VECTOR_RUNS], in_=src[:, :VECTOR_RUNS])
            nc.scalar.copy(out=dst[:, VECTOR_RUNS:], in_=src[:, VECTOR_RUNS:])
            nc.vector.quantize_mx(
                out=w_codes[z][:].bitcast(FP8X4),
                scales=w_scale[z][:],
                in_=w_bf16[z][:].rearrange("p n t -> p (n t)"),
            )

        for z in range(PASSES):
            for b in range(BLOCKS):
                nc.tensor.matmul_mx(
                    out=acc[b][:, 0, :],
                    lhsT=w_codes[z][:].bitcast(FP8X4),
                    lhsT_scale=w_scale[z][:],
                    rhs=x_codes[z][:, 2 * P * b : 2 * P * (b + 1)].bitcast(FP4X4),
                    rhs_scale=x_scale[:, z, block(b)],
                    start=(z == 0),
                    stop=(z == PASSES - 1),
                )
        y = keep.tile([P, T], F32, name="y")
        for b in range(BLOCKS):
            if b % 2 == 0:
                nc.vector.tensor_scalar_max(y[:, block(b)], acc[b][:, 0, :], 0.0)
            else:
                nc.scalar.activation(y[:, block(b)], acc[b][:, 0, :], ACT.Relu)

        last = BLOCKS - 1
        nc.tensor.transpose(acc[last][:, 2, :], gate_rows[:], ident[:])
        gate_cols = acc[last][:, 2, 0 : D * BLOCKS].rearrange("p (e b) -> p b e", e=D)
        summands = keep.tile([P, BLOCKS, D], F32, name="summands")
        stay = keep.tile([P, BLOCKS], F32, name="stay")
        for b in range(BLOCKS):
            nc.scalar.activation(
                summands[:, b, :], gate_cols[:, b, :], ACT.Copy,
                bias=1.0 / D, scale=-1.0, accum_out=stay[:, b : b + 1],
            )

        own = keep.tile([P, BLOCKS, P], F32, name="own")
        for b in range(BLOCKS):
            nc.tensor.transpose(acc[b][:, 1, :], y[:, block(b)], ident[:])
            nc.scalar.activation(own[:, b, :], acc[b][:, 1, :], ACT.Copy, scale=stay[:, b : b + 1])
        for b in range(BLOCKS):
            nc.tensor.matmul(acc[b][:, 0, :], own[:, b, :], ident[:], start=True, stop=False, is_transpose=True)

        pulled = [keep.tile([P, T], F32, name=f"pulled{d}") for d in range(D)]

        def pull(d, blocks):
            lo, hi = P * blocks[0], P * (blocks[-1] + 1)
            offsets = lists[d][:, lo // PER_COLUMN : hi // PER_COLUMN]
            nc.vector.tensor_tensor(pulled[d][:, lo:hi], y[:].indirect(offsets), gates[d][:, lo:hi], ALU.mult)

        halves = [(0, 1), (2, 3)]
        for d in range(D - 1):
            for blocks in halves if d < D - 2 else [(0, 1), (2,), (3,)]:
                pull(d, blocks)
                for b in blocks:
                    nc.tensor.matmul(
                        turn[b][:], pulled[d][:, block(b)], ident[:],
                        start=(d == 0), stop=(d == D - 2), is_transpose=True,
                    )
        three = keep.tile([P, BLOCKS, P], F32, name="three")
        for b in range(BLOCKS):
            nc.scalar.copy(three[:, b, :], turn[b][:])
            nc.tensor.matmul(acc[b][:, 0, :], three[:, b, :], ident[:], start=False, stop=True, is_transpose=True)

        for blocks in halves:
            pull(D - 1, blocks)
        result = keep.tile([P, T], F32, name="result")

        def finish(blocks, queue):
            for b in blocks:
                nc.vector.tensor_tensor(result[:, block(b)], acc[b][:, 0, :], pulled[D - 1][:, block(b)], ALU.add)
            cols = slice(P * blocks[0], P * (blocks[-1] + 1))
            queue.dma_start(out=out[:, cols], in_=result[:, cols])

        finish((0, 1), nc.sync)
        finish((2,), nc.scalar)
        finish((3,), nc.sync)
